import numpy as np
import ml_dtypes

BF16 = ml_dtypes.bfloat16


def bf(x):
    return np.asarray(x, np.float32).astype(BF16)


def f32(x):
    return np.asarray(x, np.float32)


def f64(x):
    return np.asarray(x).astype(np.float64)


def striped(idx):
    return np.tile(idx.reshape(-1, 16).T, (8, 1))


S, K, M, N, E, Q = 256, 512, 128, 256, 4, 64


def setup_inputs():
    return {"table": bf(np.random.standard_normal((K, S))), "w": bf(np.random.standard_normal((E, K, M)) / np.sqrt(K)), "c": f32(0.2 + 0.8 * np.random.random_sample((1, N))), "offs": striped(np.sort(np.random.permutation(S).reshape(E, Q), axis=1).reshape(-1))}


def reference(table, w, c, offs):
    idx = offs[:16].T.reshape(-1)
    x = f64(table)[:, idx]
    y = np.concatenate([f64(w)[e].T @ x[:, e * Q : (e + 1) * Q] for e in range(E)], axis=1)
    return y * f64(c)

@@ -1,0 +1,49 @@
+import concourse.mybir as mybir
+
+BF16, F32, U16 = mybir.dt.bfloat16, mybir.dt.float32, mybir.dt.uint16
+P = 128
+
+FLOPS = 2 * 256 * 512 * 128
+
+
+def tile_gather_matmul_kernel(tc, table, w, c, offs, out):
+    nc = tc.nc
+    K, S = table.shape
+    E, M = w.shape[0], w.shape[2]
+    N = out.shape[1]
+    Q = N // E
+    COLS = Q // 16
+    B = K // P
+
+    table_rows = table.rearrange("(p b) s -> p b s", b=B)
+    w_rows = w.rearrange("e (p b) m -> p e b m", b=B)
+
+    with (
+        tc.tile_pool(name="held", bufs=1) as held,
+        tc.psum_pool(name="psum", bufs=1) as psum,
+    ):
+        offsets = held.tile([P, N // 16], U16, name="offsets")
+        windows = [held.tile([P, 2, S], BF16, name=f"windows{h}") for h in range(B // 2)]
+        weights = held.tile([P, E, B, M], BF16, name="weights")
+        factor = held.tile([P, N], F32, name="factor")
+        result = held.tile([P, N], F32, name="result")
+
+        nc.sync.dma_start(offsets[:], offs)
+        for h in range(B // 2):
+            nc.sync.dma_start(windows[h][:], table_rows[:, 2 * h : 2 * h + 2, :])
+        nc.scalar.dma_start(weights[:], w_rows)
+        nc.scalar.dma_start(factor[:], c[0, :].partition_broadcast(P))
+
+        for e in range(E):
+            cols = slice(e * Q, (e + 1) * Q)
+            bank = psum.tile([P, Q], F32, name=f"bank{e}")
+            for b in range(B):
+                nc.tensor.matmul(
+                    bank[:],
+                    weights[:, e, b, :],
+                    windows[b // 2][:, b % 2, :].indirect(offsets[:, e * COLS : (e + 1) * COLS]),
+                    start=b == 0,
+                    stop=b == B - 1,
+                )
+            nc.vector.tensor_tensor(result[:, cols], bank[:], factor[:, cols], mybir.AluOpType.mult)
+        nc.sync.dma_start(out, result[:])

@@ -24,15 +24,16 @@ def tile_gather_matmul_kernel(tc, table, w, c, offs, out):
     ):
         offsets = held.tile([P, N // 16], U16, name="offsets")
         windows = [held.tile([P, 2, S], BF16, name=f"windows{h}") for h in range(B // 2)]
-        weights = held.tile([P, E, B, M], BF16, name="weights")
+        weights = [held.tile([P, 2, B, M], BF16, name=f"weights{h}") for h in range(E // 2)]
         factor = held.tile([P, N], F32, name="factor")
         result = held.tile([P, N], F32, name="result")
 
         nc.sync.dma_start(offsets[:], offs)
         for h in range(B // 2):
             nc.sync.dma_start(windows[h][:], table_rows[:, 2 * h : 2 * h + 2, :])
-        nc.scalar.dma_start(weights[:], w_rows)
-        nc.scalar.dma_start(factor[:], c[0, :].partition_broadcast(P))
+        nc.sync.dma_start(factor[:], c[0, :].partition_broadcast(P))
+        for h in range(E // 2):
+            nc.scalar.dma_start(weights[h][:], w_rows[:, 2 * h : 2 * h + 2])
 
         for e in range(E):
             cols = slice(e * Q, (e + 1) * Q)
@@ -40,7 +41,7 @@ def tile_gather_matmul_kernel(tc, table, w, c, offs, out):
             for b in range(B):
                 nc.tensor.matmul(
                     bank[:],
-                    weights[:, e, b, :],
+                    weights[e // 2][:, e % 2, b, :],
                     windows[b // 2][:, b % 2, :].indirect(offsets[:, e * COLS : (e + 1) * COLS]),
                     start=b == 0,
                     stop=b == B - 1,

@@ -2,6 +2,7 @@ import concourse.mybir as mybir
 
 BF16, F32, U16 = mybir.dt.bfloat16, mybir.dt.float32, mybir.dt.uint16
 P = 128
+ROWS = 32
 
 FLOPS = 2 * 256 * 512 * 128
 
@@ -26,14 +27,21 @@ def tile_gather_matmul_kernel(tc, table, w, c, offs, out):
         windows = [held.tile([P, 2, S], BF16, name=f"windows{h}") for h in range(B // 2)]
         weights = [held.tile([P, 2, B, M], BF16, name=f"weights{h}") for h in range(E // 2)]
         factor = held.tile([P, N], F32, name="factor")
+        factor_rows = held.tile([ROWS, N], F32, name="factor_rows")
+        average = held.tile([ROWS, P], F32, name="average")
         result = held.tile([P, N], F32, name="result")
 
         nc.sync.dma_start(offsets[:], offs)
         for h in range(B // 2):
             nc.sync.dma_start(windows[h][:], table_rows[:, 2 * h : 2 * h + 2, :])
-        nc.sync.dma_start(factor[:], c[0, :].partition_broadcast(P))
+        nc.scalar.dma_start(factor_rows[:], c[0, :].partition_broadcast(ROWS))
         for h in range(E // 2):
             nc.scalar.dma_start(weights[h][:], w_rows[:, 2 * h : 2 * h + 2])
+
+        nc.vector.memset(average[:], 1.0 / ROWS)
+        factor_bank = psum.tile([P, N], F32, name="factor_bank")
+        nc.tensor.matmul(factor_bank[:], average[:], factor_rows[:], start=True, stop=True)
+        nc.vector.tensor_copy(factor[:], factor_bank[:])
 
         for e in range(E):
             cols = slice(e * Q, (e + 1) * Q)

import concourse.mybir as mybir

BF16, F32, U16 = mybir.dt.bfloat16, mybir.dt.float32, mybir.dt.uint16
P = 128
ROWS = 32

FLOPS = 2 * 256 * 512 * 128


def tile_gather_matmul_kernel(tc, table, w, c, offs, out):
    nc = tc.nc
    K, S = table.shape
    E, M = w.shape[0], w.shape[2]
    N = out.shape[1]
    Q = N // E
    COLS = Q // 16
    B = K // P

    table_rows = table.rearrange("(p b) s -> p b s", b=B)
    w_rows = w.rearrange("e (p b) m -> p e b m", b=B)

    with (
        tc.tile_pool(name="held", bufs=1) as held,
        tc.psum_pool(name="psum", bufs=1) as psum,
    ):
        offsets = held.tile([P, N // 16], U16, name="offsets")
        windows = [held.tile([P, 2, S], BF16, name=f"windows{h}") for h in range(B // 2)]
        weights = [held.tile([P, 2, B, M], BF16, name=f"weights{h}") for h in range(E // 2)]
        factor = held.tile([P, N], F32, name="factor")
        factor_rows = held.tile([ROWS, N], F32, name="factor_rows")
        average = held.tile([ROWS, P], F32, name="average")
        result = held.tile([P, N], F32, name="result")

        nc.sync.dma_start(offsets[:], offs)
        for h in range(B // 2):
            nc.sync.dma_start(windows[h][:], table_rows[:, 2 * h : 2 * h + 2, :])
        nc.scalar.dma_start(factor_rows[:], c[0, :].partition_broadcast(ROWS))
        for h in range(E // 2):
            nc.scalar.dma_start(weights[h][:], w_rows[:, 2 * h : 2 * h + 2])

        nc.vector.memset(average[:], 1.0 / ROWS)
        factor_bank = psum.tile([P, N], F32, name="factor_bank")
        nc.tensor.matmul(factor_bank[:], average[:], factor_rows[:], start=True, stop=True)
        nc.vector.tensor_copy(factor[:], factor_bank[:])

        for e in range(E):
            cols = slice(e * Q, (e + 1) * Q)
            bank = psum.tile([P, Q], F32, name=f"bank{e}")
            for b in range(B):
                nc.tensor.matmul(
                    bank[:],
                    weights[e // 2][:, e % 2, b, :],
                    windows[b // 2][:, b % 2, :].indirect(offsets[:, e * COLS : (e + 1) * COLS]),
                    start=b == 0,
                    stop=b == B - 1,
                )
            nc.vector.tensor_tensor(result[:, cols], bank[:], factor[:, cols], mybir.AluOpType.mult)
        nc.sync.dma_start(out, result[:])
